import numpy as np
import ml_dtypes


def mxq(x, axis, fmt="e4m3"):
    dtype, down = {"e4m3": (ml_dtypes.float8_e4m3fn, 7), "e5m2": (ml_dtypes.float8_e5m2, 14)}[fmt]
    v = np.moveaxis(np.asarray(x, np.float32).astype(ml_dtypes.bfloat16).astype(np.float64), axis, -1)
    blocks = v.reshape(v.shape[:-1] + (-1, 32))
    amax = np.abs(blocks).max(-1, keepdims=True)
    byte = np.maximum(np.where(amax > 0, np.frexp(amax)[1] - 1 + 127, 0) - down, 1)
    scale = np.exp2(byte - 127.0)
    codes = (blocks / scale).astype(np.float32).astype(dtype).astype(np.float64)
    return np.moveaxis((codes * scale).reshape(v.shape), -1, axis)


WIDE = False


def mx_kscale(k):
    if not WIDE:
        return np.ones(k)
    levels = np.array([10, -10, 5, -5, 0])
    if k % 512:
        return np.exp2(np.random.permutation(np.resize(levels, k // 32))).repeat(32)
    a = np.empty((k // 512, 16))
    for p in range(k // 512):
        a[p, :8] = np.random.permutation(np.resize(levels, 8))
        for g in range(8):
            far = levels[np.abs(levels - a[p, g]) >= 10]
            a[p, g + 8] = far[np.random.randint(len(far))]
    return np.exp2(a.ravel()).repeat(32)


def f64(x):
    return np.asarray(x).astype(np.float64)


def striped(idx):
    return np.tile(idx.reshape(-1, 16).T, (8, 1)).astype(np.uint16)


def unstriped(offs):
    return offs[:16].T.reshape(-1).astype(np.int64)


E2M1 = np.array([0.0, 0.5, 1.0, 1.5, 2.0, 3.0, 4.0, 6.0, -0.0, -0.5, -1.0, -1.5, -2.0, -3.0, -4.0, -6.0])


def pack_weight(w, fmt):
    k, n = w.shape
    w = f64(np.asarray(w, np.float32).astype(ml_dtypes.bfloat16)).reshape(k // 32, 32, n)
    amax = np.abs(w).max(1)
    if fmt == "e4m3":
        byte = np.frexp(amax)[1] - 1 + 127 - 7
    else:
        mant, ex = np.frexp(amax / 6.0)
        byte = np.where(mant > 0.5, ex, ex - 1) + 127
    byte = np.clip(np.where(amax > 0, byte, 1), 1, 254)
    scaled = (w * np.exp2(127.0 - byte)[:, None, :]).reshape(k, n).astype(np.float32)
    by_word = np.ascontiguousarray(scaled.reshape(k // 512, 128, 4, n).transpose(0, 1, 3, 2))
    if fmt == "e4m3":
        words = by_word.astype(ml_dtypes.float8_e4m3fn).view(np.uint8)
    else:
        c = by_word.astype(ml_dtypes.float4_e2m1fn).view(np.uint8) & 0xF
        words = (c[..., 0::2] | (c[..., 1::2] << 4)).reshape(k // 512, 128, 2 * n)
    return np.ascontiguousarray(words), np.ascontiguousarray(byte.astype(np.uint8).reshape(k // 512, 16, n))


def unpack_weight(words, scales, fmt):
    g, _, n = scales.shape
    words = np.ascontiguousarray(words).reshape(g, 128, n, -1)
    if fmt == "e4m3":
        vals = words.view(ml_dtypes.float8_e4m3fn).astype(np.float64)
    else:
        nib = np.empty((g, 128, n, 4), np.uint8)
        nib[..., 0::2] = words & 0xF
        nib[..., 1::2] = words >> 4
        vals = E2M1[nib]
    vals = vals * np.repeat(np.exp2(scales.astype(np.float64) - 127.0), 8, axis=1)[..., None]
    return vals.transpose(0, 1, 3, 2).reshape(g * 512, n)


def gelu(v):
    return 0.5 * v * (1.0 + np.tanh(np.sqrt(2.0 / np.pi) * (v + 0.044715 * v**3)))


K, H, N, T, S, P1, P2, P3 = 1024, 512, 768, 4096, 2048, 1024, 512, 256


def setup_inputs():
    n = np.random.standard_normal
    s = mx_kscale(K)[:, None]
    u = mx_kscale(H)[:, None]
    tab_words, tab_scales = pack_weight(n((K, T)) * s, "e4m3")
    w1 = (0.52 * n((K, H)) / np.sqrt(K) / s).astype(np.float32)
    w2_words, w2_scales = pack_weight(1.5 * n((K, H)) / np.sqrt(K) / s * u.T, "e2m1")
    w3 = (1.2 * n((H, N)) / np.sqrt(H) / u).astype(np.float32)
    w4_words, w4_scales = pack_weight(0.9 * n((H, N)) / np.sqrt(H) / u, "e2m1")
    return {"tab_words": tab_words, "tab_scales": tab_scales,
            "offs": striped(np.random.permutation(T)[:S]),
            "pos1": striped(np.random.permutation(S)[:P1]),
            "pos2": striped(np.random.permutation(S)[:P1]),
            "pos3": striped(np.random.permutation(P1)[:P2]),
            "pos4": striped(np.random.permutation(P1)[:P2]),
            "pos5": striped(np.random.permutation(P2)[:P3]),
            "pos6": striped(np.random.permutation(P2)[:P3]),
            "w1": w1, "w2_words": w2_words, "w2_scales": w2_scales,
            "w3": w3, "w4_words": w4_words, "w4_scales": w4_scales}


def reference(tab_words, tab_scales, offs, pos1, pos2, pos3, pos4, pos5, pos6,
              w1, w2_words, w2_scales, w3, w4_words, w4_scales):
    v = unpack_weight(tab_words, tab_scales, "e4m3")[:, unstriped(offs)]
    w2 = unpack_weight(w2_words, w2_scales, "e2m1")
    w4 = unpack_weight(w4_words, w4_scales, "e2m1")
    f = np.sin(mxq(f64(w1), 0, "e4m3").T @ v)
    h = w2.T @ v
    a1 = f[:, unstriped(pos1)] * h[:, unstriped(pos2)]
    a2 = a1[:, unstriped(pos3)] - a1[:, unstriped(pos4)]
    a3 = np.maximum(a2[:, unstriped(pos5)], a2[:, unstriped(pos6)])
    aq = mxq(a3, 0, "e4m3")
    y1 = mxq(f64(w3), 0, "e4m3").T @ aq
    y2 = w4.T @ aq
    return np.tanh(y1) + np.square(y2)

@@ -1,0 +1,342 @@
+import math
+from contextlib import ExitStack
+
+import concourse.mybir as mybir
+
+K, H, N, T, S, P1, P2, P3 = 1024, 512, 768, 4096, 2048, 1024, 512, 256
+FLOPS = 2 * (2 * K * H * S + 2 * H * N * P3)
+
+F32 = mybir.dt.float32
+BF16 = mybir.dt.bfloat16
+I32 = mybir.dt.int32
+U32 = mybir.dt.uint32
+U16 = mybir.dt.uint16
+U8 = mybir.dt.uint8
+E4M3 = mybir.dt.float8_e4m3fn_x4
+E2M1 = mybir.dt.float4_e2m1fn_x4
+ALU = mybir.AluOpType
+ACT = mybir.ActivationFunctionType
+
+P = 128
+PACK = 4
+PASSES = K // (P * PACK)
+BANK = 512
+STRIPE = 16
+TURN = 2.0 * math.pi
+ANCHOR = 98304.0
+ANCHOR_BITS = 1203765248.0
+BITS_PER_TURN = 128.0
+
+
+def tile_list_stanza_longlist_features_kernel(
+    tc, tab_words, tab_scales, offs, pos1, pos2, pos3, pos4, pos5, pos6,
+    w1, w2_words, w2_scales, w3, w4_words, w4_scales, out,
+):
+    nc = tc.nc
+    with ExitStack() as ctx:
+        lists = ctx.enter_context(tc.tile_pool(name="lists", bufs=1))
+        keep = ctx.enter_context(tc.tile_pool(name="keep", bufs=1))
+        ring = ctx.enter_context(tc.tile_pool(name="ring", bufs=2))
+        psum = ctx.enter_context(tc.psum_pool(name="psum", bufs=8))
+
+        def load_list(dram, name):
+            tile = lists.tile(list(dram.shape), U16, name=name)
+            nc.sync.dma_start(tile[:], dram)
+            return tile
+
+        def load_scale_rows(tile, dram):
+            for q in range(4):
+                nc.gpsimd.dma_start(
+                    tile[32 * q : 32 * q + 4, :, :].bitcast(I32),
+                    dram[:, 4 * q : 4 * q + 4, :].rearrange("a r c -> r a c").bitcast(I32),
+                )
+
+        tab_s = keep.tile([P, T], U8, name="tab_s", align_bytes=64)
+        for q in range(4):
+            nc.sync.dma_start(tab_s[8 * q : 8 * q + 8, :].bitcast(I32), tab_scales[:, 4 * q : 4 * q + 4, :].bitcast(I32))
+        nc.vector.memset(tab_s[32:64, :].bitcast(I32), 0)
+        nc.vector.memset(tab_s[64:P, :].bitcast(I32), 0)
+        w2_s_raw = keep.tile([P, PASSES, H], U8, name="w2_s_raw", align_bytes=64)
+        nc.gpsimd.memset(w2_s_raw[:].bitcast(I32), 0)
+        v_p = keep.tile([P, S], U8, name="v_p", align_bytes=64)
+        nc.gpsimd.memset(v_p[:].bitcast(I32), 0)
+        v_p1 = keep.tile([P, S], U8, name="v_p1", align_bytes=64)
+        nc.gpsimd.memset(v_p1[:].bitcast(I32), 0)
+        w4_s = keep.tile([P, 1, N], U8, name="w4_s", align_bytes=64)
+        nc.gpsimd.memset(w4_s[:].bitcast(I32), 0)
+        offs_t = load_list(offs, "offs_t")
+        tab_w = [keep.tile([P, T], U32, name=f"tab_w{a}", align_bytes=64) for a in range(PASSES)]
+        w1_raw = [[keep.tile([P, PACK, H // 2], F32, name=f"w1_raw{a}{i}", align_bytes=64) for i in range(2)] for a in range(PASSES)]
+
+        def load_tab(a):
+            nc.sync.dma_start(tab_w[a][:].bitcast(I32), tab_words[a].rearrange("p t i -> p (t i)").bitcast(I32))
+
+        def load_w1(a):
+            for i in range(2):
+                nc.sync.dma_start(
+                    w1_raw[a][i][:],
+                    w1[a * 512 : (a + 1) * 512, i * H // 2 : (i + 1) * H // 2].rearrange("(p j) c -> p j c", j=PACK),
+                )
+
+        load_tab(0)
+        load_w1(0)
+        load_tab(1)
+        w2_raw = keep.tile([P, PASSES, 2 * H], U8, name="w2_raw", align_bytes=64)
+        nc.sync.dma_start(w2_raw[:].bitcast(I32), w2_words.rearrange("a p c -> p a c").bitcast(I32))
+        load_scale_rows(w2_s_raw, w2_scales)
+        load_scale_rows(w4_s, w4_scales)
+        p1_t = load_list(pos1, "p1_t")
+        p2_t = load_list(pos2, "p2_t")
+        p4_t = load_list(pos4, "p4_t")
+        load_w1(1)
+
+        v_s = keep.tile([P, S], U8, name="v_s", align_bytes=64)
+        nc.vector.tensor_copy(v_s[:], tab_s[:].indirect(offs_t[:]))
+        for q in range(4):
+            nc.sync.dma_start(v_p[32 * q : 32 * q + 8, :].bitcast(I32), v_s[8 * q : 8 * q + 8, :].bitcast(I32))
+        for q in range(4):
+            nc.sync.dma_start(v_p1[32 * q : 32 * q + 4, :].bitcast(I32), v_s[8 * q + 4 : 8 * q + 8, :].bitcast(I32))
+        p3_t = load_list(pos3, "p3_t")
+        p5_t = load_list(pos5, "p5_t")
+        p6_t = load_list(pos6, "p6_t")
+        w3_raw = keep.tile([P, PACK, N], F32, name="w3_raw")
+        nc.sync.dma_start(w3_raw[:], w3.rearrange("(p j) c -> p j c", j=PACK))
+        w4_w = keep.tile([P, 2 * N], U8, name="w4_w", align_bytes=64)
+        nc.sync.dma_start(w4_w[:].bitcast(I32), w4_words[0].bitcast(I32))
+
+        w2_w = keep.tile([P, PASSES, 2 * H], U8, name="w2_w", align_bytes=64)
+        w2_s = keep.tile([P, PASSES, H], U8, name="w2_s", align_bytes=64)
+        for a in range(PASSES):
+            nc.gpsimd.tensor_copy(
+                w2_w[:, a, :].rearrange("p (t m b) -> p t m b", t=PACK, b=2),
+                w2_raw[:, a, :].rearrange("p (m t b) -> p t m b", t=PACK, b=2),
+            )
+        nc.gpsimd.tensor_copy(
+            w2_s[:].rearrange("p a (t m) -> p a t m", t=PACK),
+            w2_s_raw[:].rearrange("p a (m t) -> p a t m", t=PACK),
+        )
+
+        v_w0 = keep.tile([P, S], U32, name="v_w0", align_bytes=64)
+        v_w1 = keep.tile([P, S - BANK], U32, name="v_w1", align_bytes=64)
+        v_w = {}
+        for s in range(S // BANK):
+            v_w[0, s] = v_w0[:, s * BANK : (s + 1) * BANK]
+        w1_c = [keep.tile([P, H], U32, name=f"w1_c{a}", align_bytes=64) for a in range(PASSES)]
+        w1_s = [keep.tile([P, H], U8, name=f"w1_s{a}", align_bytes=64) for a in range(PASSES)]
+        w1_b = [keep.tile([P, PACK * H], BF16, name=f"w1_b{a}", align_bytes=64) for a in range(PASSES)]
+
+        def round_w1(a):
+            for i in range(2):
+                nc.scalar.copy(
+                    w1_b[a][:].rearrange("p (t m j) -> p m t j", t=PACK, j=PACK)[:, i * P // 2 : (i + 1) * P // 2, :, :],
+                    w1_raw[a][i][:].rearrange("p j (m t) -> p m t j", t=PACK),
+                )
+
+        def quantise_w1(a, c0, c1):
+            nc.vector.quantize_mx(
+                out=w1_c[a][:, c0:c1].bitcast(E4M3), scales=w1_s[a][:, c0:c1], in_=w1_b[a][:, PACK * c0 : PACK * c1]
+            )
+
+        def gather_words(a, s):
+            if s == S // BANK - 1:
+                v_last = keep.tile([P, BANK], U32, name="v_last", tag="w1_raw11", align_bytes=64)
+                v_w[a, s] = v_last[:]
+            else:
+                v_w[a, s] = v_w1[:, s * BANK : (s + 1) * BANK]
+            nc.vector.tensor_copy(
+                v_w[a, s],
+                tab_w[a][:].indirect(offs_t[:, s * BANK // STRIPE : (s + 1) * BANK // STRIPE]),
+            )
+
+        nc.vector.tensor_copy(v_w0[:], tab_w[0][:].indirect(offs_t[:]))
+        round_w1(0)
+        round_w1(1)
+        quantise_w1(0, 0, H)
+        gather_words(1, 0)
+        gather_words(1, 1)
+        gather_words(1, 2)
+        quantise_w1(1, 0, P)
+        gather_words(1, 3)
+        quantise_w1(1, P, H)
+
+        wide = keep.tile([P, PACK, P1], F32, name="wide")
+        u5 = wide[:, :, 0:P3]
+        u6 = wide[:, :, P3 : 2 * P3]
+        y_t, h_t, g_t, r_t, s_t, a1_t, b_t, a2_t = {}, {}, {}, {}, {}, {}, {}, {}
+
+        def product_y(t, s):
+            cols = slice(s * BANK, (s + 1) * BANK)
+            if s == 0:
+                y_t[t] = keep.tile([P, S], F32, name="y", tag=f"y{t}")
+            acc = psum.tile([P, BANK], F32, name="acc")
+            for a in range(PASSES):
+                nc.tensor.matmul_mx(
+                    out=acc[:],
+                    lhsT=w1_c[a][:, t * P : (t + 1) * P].bitcast(E4M3),
+                    lhsT_scale=w1_s[a][:, t * P : (t + 1) * P],
+                    rhs=v_w[a, s].bitcast(E4M3),
+                    rhs_scale=v_p[4 * a : P, cols],
+                    start=(a == 0),
+                    stop=(a == PASSES - 1),
+                )
+            nc.scalar.activation(y_t[t][:, cols], acc[:], ACT.Copy, scale=1.0 / TURN)
+
+        def product_h(t, s):
+            cols = slice(s * BANK, (s + 1) * BANK)
+            if s == 0:
+                h_t[t] = ring.tile([P, S], F32, name="h")
+            acc = psum.tile([P, BANK], F32, name="acc")
+            for a in range(PASSES):
+                nc.tensor.matmul_mx(
+                    out=acc[:],
+                    lhsT=w2_w[:, a, 2 * t * P : 2 * (t + 1) * P].bitcast(E2M1),
+                    lhsT_scale=w2_s[:, a, t * P : (t + 1) * P],
+                    rhs=v_w[a, s].bitcast(E4M3),
+                    rhs_scale=(v_p, v_p1)[a][:, cols],
+                    start=(a == 0),
+                    stop=(a == PASSES - 1),
+                )
+            nc.scalar.copy(h_t[t][:, cols], acc[:])
+
+        def parts(t):
+            n = 2 if t == 0 else 1
+            w = P1 // n
+            return [(slice(i * w, (i + 1) * w), slice(i * w // STRIPE, (i + 1) * w // STRIPE)) for i in range(n)]
+
+        def pick_y(t):
+            if t >= 2:
+                g_t[t] = wide[:, t - 2, :]
+            else:
+                g_tile = keep.tile([P, P1], F32, name="g", tag=f"g{t}")
+                g_t[t] = g_tile[:]
+            r_t[t] = ring.tile([P, P1], U32, name="turns")
+            for cols, lc in parts(t):
+                nc.vector.tensor_copy(g_t[t][:, cols], y_t[t][:].indirect(p1_t[:, lc]))
+                nc.scalar.activation(r_t[t][:, cols], g_t[t][:, cols], ACT.Copy, bias=ANCHOR_BITS, scale=-BITS_PER_TURN)
+
+        def sine(t):
+            red = keep.tile([P, P1], F32, name="red", tag=f"x{(t + 1) % 2}")
+            s_t[t] = keep.tile([P, P1], F32, name="sn", tag=f"x{t % 2}")
+            for cols, lc in parts(t):
+                nc.vector.scalar_tensor_tensor(
+                    red[:, cols], r_t[t][:, cols].bitcast(F32), -ANCHOR, g_t[t][:, cols], ALU.add, ALU.add
+                )
+                nc.scalar.activation(s_t[t][:, cols], red[:, cols], ACT.Sin, scale=TURN)
+
+        def level1(t):
+            a1_t[t] = keep.tile([P, P1], F32, name="a1", tag=f"y{t}")
+            for cols, lc in parts(t):
+                nc.vector.tensor_tensor(a1_t[t][:, cols], h_t[t][:].indirect(p2_t[:, lc]), s_t[t][:, cols], ALU.mult)
+
+        def pick4(t):
+            if t in (1, 2):
+                b_t[t] = wide[:, t - 1, 0:P2]
+            else:
+                b_tile = keep.tile([P, P2], F32, name="b4", tag=f"g{1 - t % 2}")
+                b_t[t] = b_tile[:]
+            nc.vector.tensor_copy(b_t[t], a1_t[t][:].indirect(p4_t[:]))
+
+        def level2(t):
+            a2_t[t] = keep.tile([P, P2], F32, name="a2", tag=f"y{t + 2}")
+            nc.vector.tensor_tensor(a2_t[t][:], a1_t[t][:].indirect(p3_t[:]), b_t[t], ALU.subtract)
+
+
+        def pick5(t):
+            nc.vector.tensor_copy(u5[:, t, :], a2_t[t][:].indirect(p5_t[:]))
+
+        def pick6(t):
+            nc.vector.tensor_copy(u6[:, t, :], a2_t[t][:].indirect(p6_t[:]))
+
+        w3_b = {}
+        w3_c = keep.tile([P, N], U32, name="w3_c", align_bytes=64)
+        w3_s = keep.tile([P, N], U8, name="w3_s", align_bytes=64)
+
+        def round_w3(i):
+            cols = slice(i * N // 2, (i + 1) * N // 2)
+            w3_b[i] = keep.tile([P, N // 2, PACK], BF16, name="w3_b", tag=f"w1_raw0{i}", align_bytes=64)
+            nc.scalar.copy(
+                w3_b[i][:].rearrange("p (c i) j -> p c j i", i=4),
+                w3_raw[:, :, cols].rearrange("p j (c i) -> p c j i", i=4),
+            )
+
+        def quantise_w3(i):
+            cols = slice(i * N // 2, (i + 1) * N // 2)
+            nc.vector.quantize_mx(
+                out=w3_c[:, cols].bitcast(E4M3), scales=w3_s[:, cols],
+                in_=w3_b[i][:].rearrange("p c j -> p (c j)"),
+            )
+
+        def whole(product, t):
+            for s in range(S // BANK):
+                product(t, s)
+
+        whole(product_y, 0)
+        pick_y(0)
+        whole(product_y, 1)
+        sine(0)
+        whole(product_h, 0)
+        pick_y(1)
+        whole(product_h, 1)
+        for t in range(PACK):
+            if t + 2 < PACK:
+                whole(product_y, t + 2)
+            level1(t)
+            if t + 1 < PACK:
+                sine(t + 1)
+            pick4(t)
+            if t + 2 < PACK:
+                whole(product_h, t + 2)
+                pick_y(t + 2)
+            if t in (1, 2):
+                round_w3(t - 1)
+            if t == PACK - 1:
+                quantise_w3(0)
+            level2(t)
+            if t == PACK - 1:
+                quantise_w3(1)
+            if t >= 1:
+                pick5(t - 1)
+                pick6(t - 1)
+        pick5(PACK - 1)
+        pick6(PACK - 1)
+
+        a3_b = keep.tile([P, P3, PACK], BF16, name="a3_b", align_bytes=64)
+        nc.vector.tensor_tensor(
+            a3_b[:], u5.rearrange("p t j -> p j t"), u6.rearrange("p t j -> p j t"), ALU.max
+        )
+        a3_c = keep.tile([P, P3], U32, name="a3_c", align_bytes=64)
+        a3_s = keep.tile([P, P3], U8, name="a3_s", align_bytes=64)
+        nc.vector.quantize_mx(out=a3_c[:].bitcast(E4M3), scales=a3_s[:], in_=a3_b[:].rearrange("p j t -> p (j t)"))
+
+        for i in range(N // (2 * P)):
+            y2 = psum.tile([P, BANK], F32, name="acc")
+            y1 = psum.tile([P, BANK], F32, name="acc")
+            for u in range(2):
+                n0 = (2 * i + u) * P
+                nc.tensor.matmul_mx(
+                    out=y2[:, u * P3 : (u + 1) * P3], lhsT=w4_w[:, 2 * n0 : 2 * (n0 + P)].bitcast(E2M1),
+                    lhsT_scale=w4_s[:, 0, n0 : n0 + P], rhs=a3_c[:].bitcast(E4M3), rhs_scale=a3_s[:],
+                    start=True, stop=True,
+                )
+            for u in range(2):
+                n0 = (2 * i + u) * P
+                nc.tensor.matmul_mx(
+                    out=y1[:, u * P3 : (u + 1) * P3], lhsT=w3_c[:, n0 : n0 + P].bitcast(E4M3),
+                    lhsT_scale=w3_s[:, n0 : n0 + P], rhs=a3_c[:].bitcast(E4M3), rhs_scale=a3_s[:],
+                    start=True, stop=True,
+                )
+            th = keep.tile([P, BANK], F32, name=f"th{i}")
+            sq = keep.tile([P, BANK], F32, name=f"sq{i}")
+            res = keep.tile([P, BANK], F32, name=f"res{i}")
+            if i == 0:
+                cp = keep.tile([P, BANK], F32, name="cp")
+                nc.vector.tensor_copy(cp[:], y2[:])
+                nc.vector.tensor_tensor(sq[:], y2[:], cp[:], ALU.mult)
+            else:
+                nc.scalar.activation(sq[:], y2[:], ACT.Square)
+            nc.scalar.activation(th[:], y1[:], ACT.Tanh)
+            nc.vector.tensor_tensor(res[:], th[:], sq[:], ALU.add)
+            nc.sync.dma_start(
+                out[2 * i * P : 2 * (i + 1) * P, :].rearrange("(u p) j -> p u j", u=2),
+                res[:].rearrange("p (u j) -> p u j", u=2),
+            )

@@ -44,24 +44,22 @@ def tile_list_stanza_longlist_features_kernel(
             nc.sync.dma_start(tile[:], dram)
             return tile
 
-        def load_scale_rows(tile, dram):
+        def load_scale_rows(queue, tile, dram):
             for q in range(4):
-                nc.gpsimd.dma_start(
+                queue.dma_start(
                     tile[32 * q : 32 * q + 4, :, :].bitcast(I32),
                     dram[:, 4 * q : 4 * q + 4, :].rearrange("a r c -> r a c").bitcast(I32),
                 )
 
         tab_s = keep.tile([P, T], U8, name="tab_s", align_bytes=64)
-        for q in range(4):
-            nc.sync.dma_start(tab_s[8 * q : 8 * q + 8, :].bitcast(I32), tab_scales[:, 4 * q : 4 * q + 4, :].bitcast(I32))
+        nc.sync.dma_start(tab_s[0:32, :].bitcast(I32), tab_scales.rearrange("a q t -> (a q) t").bitcast(I32))
         nc.vector.memset(tab_s[32:64, :].bitcast(I32), 0)
         nc.vector.memset(tab_s[64:P, :].bitcast(I32), 0)
         w2_s_raw = keep.tile([P, PASSES, H], U8, name="w2_s_raw", align_bytes=64)
         nc.gpsimd.memset(w2_s_raw[:].bitcast(I32), 0)
-        v_p = keep.tile([P, S], U8, name="v_p", align_bytes=64)
-        nc.gpsimd.memset(v_p[:].bitcast(I32), 0)
-        v_p1 = keep.tile([P, S], U8, name="v_p1", align_bytes=64)
-        nc.gpsimd.memset(v_p1[:].bitcast(I32), 0)
+        v_p = [keep.tile([P, S], U8, name=f"v_p{a}", align_bytes=64) for a in range(PASSES)]
+        for a in range(PASSES):
+            nc.gpsimd.memset(v_p[a][:].bitcast(I32), 0)
         w4_s = keep.tile([P, 1, N], U8, name="w4_s", align_bytes=64)
         nc.gpsimd.memset(w4_s[:].bitcast(I32), 0)
         offs_t = load_list(offs, "offs_t")
@@ -78,24 +76,26 @@ def tile_list_stanza_longlist_features_kernel(
                     w1[a * 512 : (a + 1) * 512, i * H // 2 : (i + 1) * H // 2].rearrange("(p j) c -> p j c", j=PACK),
                 )
 
+        def move_scale_rows(queue, a, q):
+            row = 16 * a + 4 * q
+            queue.dma_start(v_p[a][32 * q : 32 * q + 4, :].bitcast(I32), v_s[row : row + 4, :].bitcast(I32))
+
         load_tab(0)
-        load_w1(0)
-        load_tab(1)
         w2_raw = keep.tile([P, PASSES, 2 * H], U8, name="w2_raw", align_bytes=64)
         nc.sync.dma_start(w2_raw[:].bitcast(I32), w2_words.rearrange("a p c -> p a c").bitcast(I32))
-        load_scale_rows(w2_s_raw, w2_scales)
-        load_scale_rows(w4_s, w4_scales)
+        load_w1(0)
         p1_t = load_list(pos1, "p1_t")
         p2_t = load_list(pos2, "p2_t")
+        load_tab(1)
         p4_t = load_list(pos4, "p4_t")
-        load_w1(1)
+        load_scale_rows(nc.gpsimd, w2_s_raw, w2_scales)
 
         v_s = keep.tile([P, S], U8, name="v_s", align_bytes=64)
         nc.vector.tensor_copy(v_s[:], tab_s[:].indirect(offs_t[:]))
-        for q in range(4):
-            nc.sync.dma_start(v_p[32 * q : 32 * q + 8, :].bitcast(I32), v_s[8 * q : 8 * q + 8, :].bitcast(I32))
-        for q in range(4):
-            nc.sync.dma_start(v_p1[32 * q : 32 * q + 4, :].bitcast(I32), v_s[8 * q + 4 : 8 * q + 8, :].bitcast(I32))
+        for a in range(PASSES):
+            for q in range(4):
+                move_scale_rows((nc.sync, nc.gpsimd)[a], a, q)
+        load_w1(1)
         p3_t = load_list(pos3, "p3_t")
         p5_t = load_list(pos5, "p5_t")
         p6_t = load_list(pos6, "p6_t")
@@ -103,18 +103,7 @@ def tile_list_stanza_longlist_features_kernel(
         nc.sync.dma_start(w3_raw[:], w3.rearrange("(p j) c -> p j c", j=PACK))
         w4_w = keep.tile([P, 2 * N], U8, name="w4_w", align_bytes=64)
         nc.sync.dma_start(w4_w[:].bitcast(I32), w4_words[0].bitcast(I32))
-
-        w2_w = keep.tile([P, PASSES, 2 * H], U8, name="w2_w", align_bytes=64)
-        w2_s = keep.tile([P, PASSES, H], U8, name="w2_s", align_bytes=64)
-        for a in range(PASSES):
-            nc.gpsimd.tensor_copy(
-                w2_w[:, a, :].rearrange("p (t m b) -> p t m b", t=PACK, b=2),
-                w2_raw[:, a, :].rearrange("p (m t b) -> p t m b", t=PACK, b=2),
-            )
-        nc.gpsimd.tensor_copy(
-            w2_s[:].rearrange("p a (t m) -> p a t m", t=PACK),
-            w2_s_raw[:].rearrange("p a (m t) -> p a t m", t=PACK),
-        )
+        load_scale_rows(nc.sync, w4_s, w4_scales)
 
         v_w0 = keep.tile([P, S], U32, name="v_w0", align_bytes=64)
         v_w1 = keep.tile([P, S - BANK], U32, name="v_w1", align_bytes=64)
@@ -152,6 +141,16 @@ def tile_list_stanza_longlist_features_kernel(
         round_w1(0)
         round_w1(1)
         quantise_w1(0, 0, H)
+        w2_w = keep.tile([P, PASSES, 2 * H], U8, name="w2_w", align_bytes=64)
+        w2_s = keep.tile([P, PASSES, H], U8, name="w2_s", tag="tab_w0", align_bytes=64)
+        nc.vector.tensor_copy(
+            w2_w[:].bitcast(U16).rearrange("p a (t m) -> p a t m", t=PACK),
+            w2_raw[:].bitcast(U16).rearrange("p a (m t) -> p a t m", t=PACK),
+        )
+        nc.vector.tensor_copy(
+            w2_s[:].rearrange("p a (t m) -> p a t m", t=PACK),
+            w2_s_raw[:].rearrange("p a (m t) -> p a t m", t=PACK),
+        )
         gather_words(1, 0)
         gather_words(1, 1)
         gather_words(1, 2)
@@ -175,11 +174,14 @@ def tile_list_stanza_longlist_features_kernel(
                     lhsT=w1_c[a][:, t * P : (t + 1) * P].bitcast(E4M3),
                     lhsT_scale=w1_s[a][:, t * P : (t + 1) * P],
                     rhs=v_w[a, s].bitcast(E4M3),
-                    rhs_scale=v_p[4 * a : P, cols],
+                    rhs_scale=v_p[a][:, cols],
                     start=(a == 0),
                     stop=(a == PASSES - 1),
                 )
-            nc.scalar.activation(y_t[t][:, cols], acc[:], ACT.Copy, scale=1.0 / TURN)
+            if t == 0 and s == S // BANK - 1:
+                nc.vector.tensor_scalar(y_t[t][:, cols], acc[:], 1.0 / TURN, None, ALU.mult)
+            else:
+                nc.scalar.activation(y_t[t][:, cols], acc[:], ACT.Copy, scale=1.0 / TURN)
 
         def product_h(t, s):
             cols = slice(s * BANK, (s + 1) * BANK)
@@ -192,7 +194,7 @@ def tile_list_stanza_longlist_features_kernel(
                     lhsT=w2_w[:, a, 2 * t * P : 2 * (t + 1) * P].bitcast(E2M1),
                     lhsT_scale=w2_s[:, a, t * P : (t + 1) * P],
                     rhs=v_w[a, s].bitcast(E4M3),
-                    rhs_scale=(v_p, v_p1)[a][:, cols],
+                    rhs_scale=v_p[a][:, cols],
                     start=(a == 0),
                     stop=(a == PASSES - 1),
                 )
@@ -232,7 +234,7 @@ def tile_list_stanza_longlist_features_kernel(
             if t in (1, 2):
                 b_t[t] = wide[:, t - 1, 0:P2]
             else:
-                b_tile = keep.tile([P, P2], F32, name="b4", tag=f"g{1 - t % 2}")
+                b_tile = keep.tile([P, P2], F32, name="b4", tag="g0")
                 b_t[t] = b_tile[:]
             nc.vector.tensor_copy(b_t[t], a1_t[t][:].indirect(p4_t[:]))
 
@@ -241,11 +243,9 @@ def tile_list_stanza_longlist_features_kernel(
             nc.vector.tensor_tensor(a2_t[t][:], a1_t[t][:].indirect(p3_t[:]), b_t[t], ALU.subtract)
 
 
-        def pick5(t):
-            nc.vector.tensor_copy(u5[:, t, :], a2_t[t][:].indirect(p5_t[:]))
-
-        def pick6(t):
-            nc.vector.tensor_copy(u6[:, t, :], a2_t[t][:].indirect(p6_t[:]))
+        def pick56(t, j0, j1):
+            for u, pos_t in ((u5, p5_t), (u6, p6_t)):
+                nc.vector.tensor_copy(u[:, t, j0:j1], a2_t[t][:].indirect(pos_t[:, j0 // STRIPE : j1 // STRIPE]))
 
         w3_b = {}
         w3_c = keep.tile([P, N], U32, name="w3_c", align_bytes=64)
@@ -272,9 +272,9 @@ def tile_list_stanza_longlist_features_kernel(
 
         whole(product_y, 0)
         pick_y(0)
-        whole(product_y, 1)
-        sine(0)
         whole(product_h, 0)
+        sine(0)
+        whole(product_y, 1)
         pick_y(1)
         whole(product_h, 1)
         for t in range(PACK):
@@ -295,48 +295,52 @@ def tile_list_stanza_longlist_features_kernel(
             if t == PACK - 1:
                 quantise_w3(1)
             if t >= 1:
-                pick5(t - 1)
-                pick6(t - 1)
-        pick5(PACK - 1)
-        pick6(PACK - 1)
+                pick56(t - 1, 0, P3)
 
-        a3_b = keep.tile([P, P3, PACK], BF16, name="a3_b", align_bytes=64)
-        nc.vector.tensor_tensor(
-            a3_b[:], u5.rearrange("p t j -> p j t"), u6.rearrange("p t j -> p j t"), ALU.max
-        )
-        a3_c = keep.tile([P, P3], U32, name="a3_c", align_bytes=64)
-        a3_s = keep.tile([P, P3], U8, name="a3_s", align_bytes=64)
-        nc.vector.quantize_mx(out=a3_c[:].bitcast(E4M3), scales=a3_s[:], in_=a3_b[:].rearrange("p j t -> p (j t)"))
-
-        for i in range(N // (2 * P)):
-            y2 = psum.tile([P, BANK], F32, name="acc")
-            y1 = psum.tile([P, BANK], F32, name="acc")
-            for u in range(2):
-                n0 = (2 * i + u) * P
-                nc.tensor.matmul_mx(
-                    out=y2[:, u * P3 : (u + 1) * P3], lhsT=w4_w[:, 2 * n0 : 2 * (n0 + P)].bitcast(E2M1),
-                    lhsT_scale=w4_s[:, 0, n0 : n0 + P], rhs=a3_c[:].bitcast(E4M3), rhs_scale=a3_s[:],
-                    start=True, stop=True,
-                )
-            for u in range(2):
-                n0 = (2 * i + u) * P
-                nc.tensor.matmul_mx(
-                    out=y1[:, u * P3 : (u + 1) * P3], lhsT=w3_c[:, n0 : n0 + P].bitcast(E4M3),
-                    lhsT_scale=w3_s[:, n0 : n0 + P], rhs=a3_c[:].bitcast(E4M3), rhs_scale=a3_s[:],
-                    start=True, stop=True,
-                )
-            th = keep.tile([P, BANK], F32, name=f"th{i}")
-            sq = keep.tile([P, BANK], F32, name=f"sq{i}")
-            res = keep.tile([P, BANK], F32, name=f"res{i}")
-            if i == 0:
-                cp = keep.tile([P, BANK], F32, name="cp")
-                nc.vector.tensor_copy(cp[:], y2[:])
-                nc.vector.tensor_tensor(sq[:], y2[:], cp[:], ALU.mult)
-            else:
-                nc.scalar.activation(sq[:], y2[:], ACT.Square)
-            nc.scalar.activation(th[:], y1[:], ACT.Tanh)
-            nc.vector.tensor_tensor(res[:], th[:], sq[:], ALU.add)
-            nc.sync.dma_start(
-                out[2 * i * P : 2 * (i + 1) * P, :].rearrange("(u p) j -> p u j", u=2),
-                res[:].rearrange("p (u j) -> p u j", u=2),
+        half = P3 // 2
+        group = 3
+        staged = {}
+        for c in range(2):
+            js = slice(c * half, (c + 1) * half)
+            pick56(PACK - 1, c * half, (c + 1) * half)
+            a3_b = keep.tile([P, half, PACK], BF16, name=f"a3_b{c}", align_bytes=64)
+            nc.vector.tensor_tensor(
+                a3_b[:].rearrange("p (c i) t -> p c t i", i=4),
+                u5[:, :, js].rearrange("p t (c i) -> p c t i", i=4),
+                u6[:, :, js].rearrange("p t (c i) -> p c t i", i=4),
+                ALU.max,
             )
+            a3_c = keep.tile([P, half], U32, name=f"a3_c{c}", align_bytes=64)
+            a3_s = keep.tile([P, half], U8, name=f"a3_s{c}", align_bytes=64)
+            nc.vector.quantize_mx(out=a3_c[:].bitcast(E4M3), scales=a3_s[:], in_=a3_b[:].rearrange("p j t -> p (j t)"))
+            for i in range(N // (group * P)):
+                y2 = psum.tile([P, BANK], F32, name="acc")
+                y1 = psum.tile([P, BANK], F32, name="acc")
+                for u in range(group):
+                    n0 = (group * i + u) * P
+                    nc.tensor.matmul_mx(
+                        out=y1[:, u * half : (u + 1) * half], lhsT=w3_c[:, n0 : n0 + P].bitcast(E4M3),
+                        lhsT_scale=w3_s[:, n0 : n0 + P], rhs=a3_c[:].bitcast(E4M3), rhs_scale=a3_s[:],
+                        start=True, stop=True,
+                    )
+                for u in range(group):
+                    n0 = (group * i + u) * P
+                    nc.tensor.matmul_mx(
+                        out=y2[:, u * half : (u + 1) * half], lhsT=w4_w[:, 2 * n0 : 2 * (n0 + P)].bitcast(E2M1),
+                        lhsT_scale=w4_s[:, 0, n0 : n0 + P], rhs=a3_c[:].bitcast(E4M3), rhs_scale=a3_s[:],
+                        start=True, stop=True,
+                    )
+                th = keep.tile([P, group * half], F32, name=f"th{c}{i}")
+                sq = keep.tile([P, group * half], F32, name=f"sq{c}{i}")
+                nc.scalar.activation(th[:], y1[:, 0 : group * half], ACT.Tanh)
+                nc.scalar.activation(sq[:], y2[:, 0 : group * half], ACT.Square)
+                staged[c, i] = (th, sq)
+        for c in range(2):
+            for i in range(N // (group * P)):
+                th, sq = staged[c, i]
+                res = keep.tile([P, group * half], F32, name=f"res{c}{i}")
+                nc.vector.tensor_tensor(res[:], th[:], sq[:], ALU.add)
+                nc.sync.dma_start(
+                    out[group * i * P : group * (i + 1) * P, c * half : (c + 1) * half].rearrange("(u p) j -> p u j", u=group),
+                    res[:].rearrange("p (u j) -> p u j", u=group),
+                )

@@ -200,11 +200,6 @@ def tile_list_stanza_longlist_features_kernel(
                 )
             nc.scalar.copy(h_t[t][:, cols], acc[:])
 
-        def parts(t):
-            n = 2 if t == 0 else 1
-            w = P1 // n
-            return [(slice(i * w, (i + 1) * w), slice(i * w // STRIPE, (i + 1) * w // STRIPE)) for i in range(n)]
-
         def pick_y(t):
             if t >= 2:
                 g_t[t] = wide[:, t - 2, :]
@@ -212,29 +207,27 @@ def tile_list_stanza_longlist_features_kernel(
                 g_tile = keep.tile([P, P1], F32, name="g", tag=f"g{t}")
                 g_t[t] = g_tile[:]
             r_t[t] = ring.tile([P, P1], U32, name="turns")
-            for cols, lc in parts(t):
-                nc.vector.tensor_copy(g_t[t][:, cols], y_t[t][:].indirect(p1_t[:, lc]))
-                nc.scalar.activation(r_t[t][:, cols], g_t[t][:, cols], ACT.Copy, bias=ANCHOR_BITS, scale=-BITS_PER_TURN)
+            nc.vector.tensor_copy(g_t[t], y_t[t][:].indirect(p1_t[:]))
+            if t == 0:
+                nc.vector.tensor_scalar(r_t[t][:].bitcast(I32), g_t[t], -BITS_PER_TURN, ANCHOR_BITS, ALU.mult, ALU.add)
+            else:
+                nc.scalar.activation(r_t[t][:], g_t[t], ACT.Copy, bias=ANCHOR_BITS, scale=-BITS_PER_TURN)
 
         def sine(t):
             red = keep.tile([P, P1], F32, name="red", tag=f"x{(t + 1) % 2}")
             s_t[t] = keep.tile([P, P1], F32, name="sn", tag=f"x{t % 2}")
-            for cols, lc in parts(t):
-                nc.vector.scalar_tensor_tensor(
-                    red[:, cols], r_t[t][:, cols].bitcast(F32), -ANCHOR, g_t[t][:, cols], ALU.add, ALU.add
-                )
-                nc.scalar.activation(s_t[t][:, cols], red[:, cols], ACT.Sin, scale=TURN)
+            nc.vector.scalar_tensor_tensor(red[:], r_t[t][:].bitcast(F32), -ANCHOR, g_t[t], ALU.add, ALU.add)
+            nc.scalar.activation(s_t[t][:], red[:], ACT.Sin, scale=TURN)
 
         def level1(t):
             a1_t[t] = keep.tile([P, P1], F32, name="a1", tag=f"y{t}")
-            for cols, lc in parts(t):
-                nc.vector.tensor_tensor(a1_t[t][:, cols], h_t[t][:].indirect(p2_t[:, lc]), s_t[t][:, cols], ALU.mult)
+            nc.vector.tensor_tensor(a1_t[t][:], h_t[t][:].indirect(p2_t[:]), s_t[t][:], ALU.mult)
 
         def pick4(t):
             if t in (1, 2):
                 b_t[t] = wide[:, t - 1, 0:P2]
             else:
-                b_tile = keep.tile([P, P2], F32, name="b4", tag="g0")
+                b_tile = keep.tile([P, P2], F32, name="b4", tag=f"g{1 - t % 2}")
                 b_t[t] = b_tile[:]
             nc.vector.tensor_copy(b_t[t], a1_t[t][:].indirect(p4_t[:]))
 
@@ -272,20 +265,19 @@ def tile_list_stanza_longlist_features_kernel(
 
         whole(product_y, 0)
         pick_y(0)
+        whole(product_y, 1)
         whole(product_h, 0)
         sine(0)
-        whole(product_y, 1)
         pick_y(1)
-        whole(product_h, 1)
         for t in range(PACK):
             if t + 2 < PACK:
                 whole(product_y, t + 2)
             level1(t)
             if t + 1 < PACK:
                 sine(t + 1)
+                whole(product_h, t + 1)
             pick4(t)
             if t + 2 < PACK:
-                whole(product_h, t + 2)
                 pick_y(t + 2)
             if t in (1, 2):
                 round_w3(t - 1)

@@ -186,7 +186,7 @@ def tile_list_stanza_longlist_features_kernel(
         def product_h(t, s):
             cols = slice(s * BANK, (s + 1) * BANK)
             if s == 0:
-                h_t[t] = ring.tile([P, S], F32, name="h")
+                h_t[t] = keep.tile([P, S], F32, name="h", tag=f"h{t % 2}")
             acc = psum.tile([P, BANK], F32, name="acc")
             for a in range(PASSES):
                 nc.tensor.matmul_mx(
@@ -201,34 +201,33 @@ def tile_list_stanza_longlist_features_kernel(
             nc.scalar.copy(h_t[t][:, cols], acc[:])
 
         def pick_y(t):
-            if t >= 2:
-                g_t[t] = wide[:, t - 2, :]
-            else:
-                g_tile = keep.tile([P, P1], F32, name="g", tag=f"g{t}")
-                g_t[t] = g_tile[:]
-            r_t[t] = ring.tile([P, P1], U32, name="turns")
-            nc.vector.tensor_copy(g_t[t], y_t[t][:].indirect(p1_t[:]))
+            g_t[t] = ring.tile([P, P1], F32, name="g")
+            turns = ring.tile([P, P1], U32, name="turns")
+            nc.vector.tensor_copy(g_t[t][:], y_t[t][:].indirect(p1_t[:]))
             if t == 0:
-                nc.vector.tensor_scalar(r_t[t][:].bitcast(I32), g_t[t], -BITS_PER_TURN, ANCHOR_BITS, ALU.mult, ALU.add)
+                nc.vector.tensor_scalar(turns[:].bitcast(I32), g_t[t][:], -BITS_PER_TURN, ANCHOR_BITS, ALU.mult, ALU.add)
+                r_t[t] = turns
             else:
-                nc.scalar.activation(r_t[t][:], g_t[t], ACT.Copy, bias=ANCHOR_BITS, scale=-BITS_PER_TURN)
+                nc.scalar.activation(turns[:], g_t[t][:], ACT.Copy, bias=ANCHOR_BITS, scale=-BITS_PER_TURN)
+                r_t[t] = ring.tile([P, P1], F32, name="minus_turns")
+                nc.scalar.activation(r_t[t][:], turns[:].bitcast(F32), ACT.Copy, bias=-ANCHOR)
 
         def sine(t):
-            red = keep.tile([P, P1], F32, name="red", tag=f"x{(t + 1) % 2}")
-            s_t[t] = keep.tile([P, P1], F32, name="sn", tag=f"x{t % 2}")
-            nc.vector.scalar_tensor_tensor(red[:], r_t[t][:].bitcast(F32), -ANCHOR, g_t[t], ALU.add, ALU.add)
-            nc.scalar.activation(s_t[t][:], red[:], ACT.Sin, scale=TURN)
+            red = keep.tile([P, P1], F32, name="red", tag=f"h{(t - 1) % 2}")
+            s_t[t] = wide[:, (t - 1) % PACK, :]
+            if t == 0:
+                nc.vector.scalar_tensor_tensor(red[:], r_t[t][:].bitcast(F32), -ANCHOR, g_t[t][:], ALU.add, ALU.add)
+            else:
+                nc.gpsimd.tensor_tensor(red[:], r_t[t][:], g_t[t][:], ALU.add)
+            nc.scalar.activation(s_t[t], red[:], ACT.Sin, scale=TURN)
 
         def level1(t):
             a1_t[t] = keep.tile([P, P1], F32, name="a1", tag=f"y{t}")
-            nc.vector.tensor_tensor(a1_t[t][:], h_t[t][:].indirect(p2_t[:]), s_t[t][:], ALU.mult)
+            nc.vector.tensor_tensor(a1_t[t][:], h_t[t][:].indirect(p2_t[:]), s_t[t], ALU.mult)
 
         def pick4(t):
-            if t in (1, 2):
-                b_t[t] = wide[:, t - 1, 0:P2]
-            else:
-                b_tile = keep.tile([P, P2], F32, name="b4", tag=f"g{1 - t % 2}")
-                b_t[t] = b_tile[:]
+            b_tile = keep.tile([P, P2], F32, name="b4", tag=f"y{t + 1}")
+            b_t[t] = b_tile[:]
             nc.vector.tensor_copy(b_t[t], a1_t[t][:].indirect(p4_t[:]))
 
         def level2(t):
@@ -268,26 +267,35 @@ def tile_list_stanza_longlist_features_kernel(
         whole(product_y, 1)
         whole(product_h, 0)
         sine(0)
+        product_y(2, 0)
+        product_y(2, 1)
         pick_y(1)
+        product_y(2, 2)
+        product_y(2, 3)
+        whole(product_h, 1)
         for t in range(PACK):
-            if t + 2 < PACK:
-                whole(product_y, t + 2)
             level1(t)
             if t + 1 < PACK:
                 sine(t + 1)
-                whole(product_h, t + 1)
+            if t == 1:
+                whole(product_h, 2)
+            if t == 2:
+                round_w3(0)
+                round_w3(1)
+            if t >= 1:
+                pick56(t - 1, 0, P3)
             pick4(t)
             if t + 2 < PACK:
                 pick_y(t + 2)
-            if t in (1, 2):
-                round_w3(t - 1)
             if t == PACK - 1:
                 quantise_w3(0)
             level2(t)
+            if t == 0:
+                whole(product_y, 3)
+            if t == 1:
+                whole(product_h, 3)
             if t == PACK - 1:
                 quantise_w3(1)
-            if t >= 1:
-                pick56(t - 1, 0, P3)
 
         half = P3 // 2
         group = 3

@@ -62,6 +62,10 @@ def tile_list_stanza_longlist_features_kernel(
             nc.gpsimd.memset(v_p[a][:].bitcast(I32), 0)
         w4_s = keep.tile([P, 1, N], U8, name="w4_s", align_bytes=64)
         nc.gpsimd.memset(w4_s[:].bitcast(I32), 0)
+        warm_in = keep.tile([P, 1], F32, name="warm_in")
+        warm_out = keep.tile([P, 1], F32, name="warm_out")
+        nc.gpsimd.memset(warm_in[:], 0.0)
+        nc.scalar.activation(warm_out[:], warm_in[:], ACT.Sin, scale=TURN)
         offs_t = load_list(offs, "offs_t")
         tab_w = [keep.tile([P, T], U32, name=f"tab_w{a}", align_bytes=64) for a in range(PASSES)]
         w1_raw = [[keep.tile([P, PACK, H // 2], F32, name=f"w1_raw{a}{i}", align_bytes=64) for i in range(2)] for a in range(PASSES)]

import math
from contextlib import ExitStack

import concourse.mybir as mybir

K, H, N, T, S, P1, P2, P3 = 1024, 512, 768, 4096, 2048, 1024, 512, 256
FLOPS = 2 * (2 * K * H * S + 2 * H * N * P3)

F32 = mybir.dt.float32
BF16 = mybir.dt.bfloat16
I32 = mybir.dt.int32
U32 = mybir.dt.uint32
U16 = mybir.dt.uint16
U8 = mybir.dt.uint8
E4M3 = mybir.dt.float8_e4m3fn_x4
E2M1 = mybir.dt.float4_e2m1fn_x4
ALU = mybir.AluOpType
ACT = mybir.ActivationFunctionType

P = 128
PACK = 4
PASSES = K // (P * PACK)
BANK = 512
STRIPE = 16
TURN = 2.0 * math.pi
ANCHOR = 98304.0
ANCHOR_BITS = 1203765248.0
BITS_PER_TURN = 128.0


def tile_list_stanza_longlist_features_kernel(
    tc, tab_words, tab_scales, offs, pos1, pos2, pos3, pos4, pos5, pos6,
    w1, w2_words, w2_scales, w3, w4_words, w4_scales, out,
):
    nc = tc.nc
    with ExitStack() as ctx:
        lists = ctx.enter_context(tc.tile_pool(name="lists", bufs=1))
        keep = ctx.enter_context(tc.tile_pool(name="keep", bufs=1))
        ring = ctx.enter_context(tc.tile_pool(name="ring", bufs=2))
        psum = ctx.enter_context(tc.psum_pool(name="psum", bufs=8))

        def load_list(dram, name):
            tile = lists.tile(list(dram.shape), U16, name=name)
            nc.sync.dma_start(tile[:], dram)
            return tile

        def load_scale_rows(queue, tile, dram):
            for q in range(4):
                queue.dma_start(
                    tile[32 * q : 32 * q + 4, :, :].bitcast(I32),
                    dram[:, 4 * q : 4 * q + 4, :].rearrange("a r c -> r a c").bitcast(I32),
                )

        tab_s = keep.tile([P, T], U8, name="tab_s", align_bytes=64)
        nc.sync.dma_start(tab_s[0:32, :].bitcast(I32), tab_scales.rearrange("a q t -> (a q) t").bitcast(I32))
        nc.vector.memset(tab_s[32:64, :].bitcast(I32), 0)
        nc.vector.memset(tab_s[64:P, :].bitcast(I32), 0)
        w2_s_raw = keep.tile([P, PASSES, H], U8, name="w2_s_raw", align_bytes=64)
        nc.gpsimd.memset(w2_s_raw[:].bitcast(I32), 0)
        v_p = [keep.tile([P, S], U8, name=f"v_p{a}", align_bytes=64) for a in range(PASSES)]
        for a in range(PASSES):
            nc.gpsimd.memset(v_p[a][:].bitcast(I32), 0)
        w4_s = keep.tile([P, 1, N], U8, name="w4_s", align_bytes=64)
        nc.gpsimd.memset(w4_s[:].bitcast(I32), 0)
        warm_in = keep.tile([P, 1], F32, name="warm_in")
        warm_out = keep.tile([P, 1], F32, name="warm_out")
        nc.gpsimd.memset(warm_in[:], 0.0)
        nc.scalar.activation(warm_out[:], warm_in[:], ACT.Sin, scale=TURN)
        offs_t = load_list(offs, "offs_t")
        tab_w = [keep.tile([P, T], U32, name=f"tab_w{a}", align_bytes=64) for a in range(PASSES)]
        w1_raw = [[keep.tile([P, PACK, H // 2], F32, name=f"w1_raw{a}{i}", align_bytes=64) for i in range(2)] for a in range(PASSES)]

        def load_tab(a):
            nc.sync.dma_start(tab_w[a][:].bitcast(I32), tab_words[a].rearrange("p t i -> p (t i)").bitcast(I32))

        def load_w1(a):
            for i in range(2):
                nc.sync.dma_start(
                    w1_raw[a][i][:],
                    w1[a * 512 : (a + 1) * 512, i * H // 2 : (i + 1) * H // 2].rearrange("(p j) c -> p j c", j=PACK),
                )

        def move_scale_rows(queue, a, q):
            row = 16 * a + 4 * q
            queue.dma_start(v_p[a][32 * q : 32 * q + 4, :].bitcast(I32), v_s[row : row + 4, :].bitcast(I32))

        load_tab(0)
        w2_raw = keep.tile([P, PASSES, 2 * H], U8, name="w2_raw", align_bytes=64)
        nc.sync.dma_start(w2_raw[:].bitcast(I32), w2_words.rearrange("a p c -> p a c").bitcast(I32))
        load_w1(0)
        p1_t = load_list(pos1, "p1_t")
        p2_t = load_list(pos2, "p2_t")
        load_tab(1)
        p4_t = load_list(pos4, "p4_t")
        load_scale_rows(nc.gpsimd, w2_s_raw, w2_scales)

        v_s = keep.tile([P, S], U8, name="v_s", align_bytes=64)
        nc.vector.tensor_copy(v_s[:], tab_s[:].indirect(offs_t[:]))
        for a in range(PASSES):
            for q in range(4):
                move_scale_rows((nc.sync, nc.gpsimd)[a], a, q)
        load_w1(1)
        p3_t = load_list(pos3, "p3_t")
        p5_t = load_list(pos5, "p5_t")
        p6_t = load_list(pos6, "p6_t")
        w3_raw = keep.tile([P, PACK, N], F32, name="w3_raw")
        nc.sync.dma_start(w3_raw[:], w3.rearrange("(p j) c -> p j c", j=PACK))
        w4_w = keep.tile([P, 2 * N], U8, name="w4_w", align_bytes=64)
        nc.sync.dma_start(w4_w[:].bitcast(I32), w4_words[0].bitcast(I32))
        load_scale_rows(nc.sync, w4_s, w4_scales)

        v_w0 = keep.tile([P, S], U32, name="v_w0", align_bytes=64)
        v_w1 = keep.tile([P, S - BANK], U32, name="v_w1", align_bytes=64)
        v_w = {}
        for s in range(S // BANK):
            v_w[0, s] = v_w0[:, s * BANK : (s + 1) * BANK]
        w1_c = [keep.tile([P, H], U32, name=f"w1_c{a}", align_bytes=64) for a in range(PASSES)]
        w1_s = [keep.tile([P, H], U8, name=f"w1_s{a}", align_bytes=64) for a in range(PASSES)]
        w1_b = [keep.tile([P, PACK * H], BF16, name=f"w1_b{a}", align_bytes=64) for a in range(PASSES)]

        def round_w1(a):
            for i in range(2):
                nc.scalar.copy(
                    w1_b[a][:].rearrange("p (t m j) -> p m t j", t=PACK, j=PACK)[:, i * P // 2 : (i + 1) * P // 2, :, :],
                    w1_raw[a][i][:].rearrange("p j (m t) -> p m t j", t=PACK),
                )

        def quantise_w1(a, c0, c1):
            nc.vector.quantize_mx(
                out=w1_c[a][:, c0:c1].bitcast(E4M3), scales=w1_s[a][:, c0:c1], in_=w1_b[a][:, PACK * c0 : PACK * c1]
            )

        def gather_words(a, s):
            if s == S // BANK - 1:
                v_last = keep.tile([P, BANK], U32, name="v_last", tag="w1_raw11", align_bytes=64)
                v_w[a, s] = v_last[:]
            else:
                v_w[a, s] = v_w1[:, s * BANK : (s + 1) * BANK]
            nc.vector.tensor_copy(
                v_w[a, s],
                tab_w[a][:].indirect(offs_t[:, s * BANK // STRIPE : (s + 1) * BANK // STRIPE]),
            )

        nc.vector.tensor_copy(v_w0[:], tab_w[0][:].indirect(offs_t[:]))
        round_w1(0)
        round_w1(1)
        quantise_w1(0, 0, H)
        w2_w = keep.tile([P, PASSES, 2 * H], U8, name="w2_w", align_bytes=64)
        w2_s = keep.tile([P, PASSES, H], U8, name="w2_s", tag="tab_w0", align_bytes=64)
        nc.vector.tensor_copy(
            w2_w[:].bitcast(U16).rearrange("p a (t m) -> p a t m", t=PACK),
            w2_raw[:].bitcast(U16).rearrange("p a (m t) -> p a t m", t=PACK),
        )
        nc.vector.tensor_copy(
            w2_s[:].rearrange("p a (t m) -> p a t m", t=PACK),
            w2_s_raw[:].rearrange("p a (m t) -> p a t m", t=PACK),
        )
        gather_words(1, 0)
        gather_words(1, 1)
        gather_words(1, 2)
        quantise_w1(1, 0, P)
        gather_words(1, 3)
        quantise_w1(1, P, H)

        wide = keep.tile([P, PACK, P1], F32, name="wide")
        u5 = wide[:, :, 0:P3]
        u6 = wide[:, :, P3 : 2 * P3]
        y_t, h_t, g_t, r_t, s_t, a1_t, b_t, a2_t = {}, {}, {}, {}, {}, {}, {}, {}

        def product_y(t, s):
            cols = slice(s * BANK, (s + 1) * BANK)
            if s == 0:
                y_t[t] = keep.tile([P, S], F32, name="y", tag=f"y{t}")
            acc = psum.tile([P, BANK], F32, name="acc")
            for a in range(PASSES):
                nc.tensor.matmul_mx(
                    out=acc[:],
                    lhsT=w1_c[a][:, t * P : (t + 1) * P].bitcast(E4M3),
                    lhsT_scale=w1_s[a][:, t * P : (t + 1) * P],
                    rhs=v_w[a, s].bitcast(E4M3),
                    rhs_scale=v_p[a][:, cols],
                    start=(a == 0),
                    stop=(a == PASSES - 1),
                )
            if t == 0 and s == S // BANK - 1:
                nc.vector.tensor_scalar(y_t[t][:, cols], acc[:], 1.0 / TURN, None, ALU.mult)
            else:
                nc.scalar.activation(y_t[t][:, cols], acc[:], ACT.Copy, scale=1.0 / TURN)

        def product_h(t, s):
            cols = slice(s * BANK, (s + 1) * BANK)
            if s == 0:
                h_t[t] = keep.tile([P, S], F32, name="h", tag=f"h{t % 2}")
            acc = psum.tile([P, BANK], F32, name="acc")
            for a in range(PASSES):
                nc.tensor.matmul_mx(
                    out=acc[:],
                    lhsT=w2_w[:, a, 2 * t * P : 2 * (t + 1) * P].bitcast(E2M1),
                    lhsT_scale=w2_s[:, a, t * P : (t + 1) * P],
                    rhs=v_w[a, s].bitcast(E4M3),
                    rhs_scale=v_p[a][:, cols],
                    start=(a == 0),
                    stop=(a == PASSES - 1),
                )
            nc.scalar.copy(h_t[t][:, cols], acc[:])

        def pick_y(t):
            g_t[t] = ring.tile([P, P1], F32, name="g")
            turns = ring.tile([P, P1], U32, name="turns")
            nc.vector.tensor_copy(g_t[t][:], y_t[t][:].indirect(p1_t[:]))
            if t == 0:
                nc.vector.tensor_scalar(turns[:].bitcast(I32), g_t[t][:], -BITS_PER_TURN, ANCHOR_BITS, ALU.mult, ALU.add)
                r_t[t] = turns
            else:
                nc.scalar.activation(turns[:], g_t[t][:], ACT.Copy, bias=ANCHOR_BITS, scale=-BITS_PER_TURN)
                r_t[t] = ring.tile([P, P1], F32, name="minus_turns")
                nc.scalar.activation(r_t[t][:], turns[:].bitcast(F32), ACT.Copy, bias=-ANCHOR)

        def sine(t):
            red = keep.tile([P, P1], F32, name="red", tag=f"h{(t - 1) % 2}")
            s_t[t] = wide[:, (t - 1) % PACK, :]
            if t == 0:
                nc.vector.scalar_tensor_tensor(red[:], r_t[t][:].bitcast(F32), -ANCHOR, g_t[t][:], ALU.add, ALU.add)
            else:
                nc.gpsimd.tensor_tensor(red[:], r_t[t][:], g_t[t][:], ALU.add)
            nc.scalar.activation(s_t[t], red[:], ACT.Sin, scale=TURN)

        def level1(t):
            a1_t[t] = keep.tile([P, P1], F32, name="a1", tag=f"y{t}")
            nc.vector.tensor_tensor(a1_t[t][:], h_t[t][:].indirect(p2_t[:]), s_t[t], ALU.mult)

        def pick4(t):
            b_tile = keep.tile([P, P2], F32, name="b4", tag=f"y{t + 1}")
            b_t[t] = b_tile[:]
            nc.vector.tensor_copy(b_t[t], a1_t[t][:].indirect(p4_t[:]))

        def level2(t):
            a2_t[t] = keep.tile([P, P2], F32, name="a2", tag=f"y{t + 2}")
            nc.vector.tensor_tensor(a2_t[t][:], a1_t[t][:].indirect(p3_t[:]), b_t[t], ALU.subtract)


        def pick56(t, j0, j1):
            for u, pos_t in ((u5, p5_t), (u6, p6_t)):
                nc.vector.tensor_copy(u[:, t, j0:j1], a2_t[t][:].indirect(pos_t[:, j0 // STRIPE : j1 // STRIPE]))

        w3_b = {}
        w3_c = keep.tile([P, N], U32, name="w3_c", align_bytes=64)
        w3_s = keep.tile([P, N], U8, name="w3_s", align_bytes=64)

        def round_w3(i):
            cols = slice(i * N // 2, (i + 1) * N // 2)
            w3_b[i] = keep.tile([P, N // 2, PACK], BF16, name="w3_b", tag=f"w1_raw0{i}", align_bytes=64)
            nc.scalar.copy(
                w3_b[i][:].rearrange("p (c i) j -> p c j i", i=4),
                w3_raw[:, :, cols].rearrange("p j (c i) -> p c j i", i=4),
            )

        def quantise_w3(i):
            cols = slice(i * N // 2, (i + 1) * N // 2)
            nc.vector.quantize_mx(
                out=w3_c[:, cols].bitcast(E4M3), scales=w3_s[:, cols],
                in_=w3_b[i][:].rearrange("p c j -> p (c j)"),
            )

        def whole(product, t):
            for s in range(S // BANK):
                product(t, s)

        whole(product_y, 0)
        pick_y(0)
        whole(product_y, 1)
        whole(product_h, 0)
        sine(0)
        product_y(2, 0)
        product_y(2, 1)
        pick_y(1)
        product_y(2, 2)
        product_y(2, 3)
        whole(product_h, 1)
        for t in range(PACK):
            level1(t)
            if t + 1 < PACK:
                sine(t + 1)
            if t == 1:
                whole(product_h, 2)
            if t == 2:
                round_w3(0)
                round_w3(1)
            if t >= 1:
                pick56(t - 1, 0, P3)
            pick4(t)
            if t + 2 < PACK:
                pick_y(t + 2)
            if t == PACK - 1:
                quantise_w3(0)
            level2(t)
            if t == 0:
                whole(product_y, 3)
            if t == 1:
                whole(product_h, 3)
            if t == PACK - 1:
                quantise_w3(1)

        half = P3 // 2
        group = 3
        staged = {}
        for c in range(2):
            js = slice(c * half, (c + 1) * half)
            pick56(PACK - 1, c * half, (c + 1) * half)
            a3_b = keep.tile([P, half, PACK], BF16, name=f"a3_b{c}", align_bytes=64)
            nc.vector.tensor_tensor(
                a3_b[:].rearrange("p (c i) t -> p c t i", i=4),
                u5[:, :, js].rearrange("p t (c i) -> p c t i", i=4),
                u6[:, :, js].rearrange("p t (c i) -> p c t i", i=4),
                ALU.max,
            )
            a3_c = keep.tile([P, half], U32, name=f"a3_c{c}", align_bytes=64)
            a3_s = keep.tile([P, half], U8, name=f"a3_s{c}", align_bytes=64)
            nc.vector.quantize_mx(out=a3_c[:].bitcast(E4M3), scales=a3_s[:], in_=a3_b[:].rearrange("p j t -> p (j t)"))
            for i in range(N // (group * P)):
                y2 = psum.tile([P, BANK], F32, name="acc")
                y1 = psum.tile([P, BANK], F32, name="acc")
                for u in range(group):
                    n0 = (group * i + u) * P
                    nc.tensor.matmul_mx(
                        out=y1[:, u * half : (u + 1) * half], lhsT=w3_c[:, n0 : n0 + P].bitcast(E4M3),
                        lhsT_scale=w3_s[:, n0 : n0 + P], rhs=a3_c[:].bitcast(E4M3), rhs_scale=a3_s[:],
                        start=True, stop=True,
                    )
                for u in range(group):
                    n0 = (group * i + u) * P
                    nc.tensor.matmul_mx(
                        out=y2[:, u * half : (u + 1) * half], lhsT=w4_w[:, 2 * n0 : 2 * (n0 + P)].bitcast(E2M1),
                        lhsT_scale=w4_s[:, 0, n0 : n0 + P], rhs=a3_c[:].bitcast(E4M3), rhs_scale=a3_s[:],
                        start=True, stop=True,
                    )
                th = keep.tile([P, group * half], F32, name=f"th{c}{i}")
                sq = keep.tile([P, group * half], F32, name=f"sq{c}{i}")
                nc.scalar.activation(th[:], y1[:, 0 : group * half], ACT.Tanh)
                nc.scalar.activation(sq[:], y2[:, 0 : group * half], ACT.Square)
                staged[c, i] = (th, sq)
        for c in range(2):
            for i in range(N // (group * P)):
                th, sq = staged[c, i]
                res = keep.tile([P, group * half], F32, name=f"res{c}{i}")
                nc.vector.tensor_tensor(res[:], th[:], sq[:], ALU.add)
                nc.sync.dma_start(
                    out[group * i * P : group * (i + 1) * P, c * half : (c + 1) * half].rearrange("(u p) j -> p u j", u=group),
                    res[:].rearrange("p (u j) -> p u j", u=group),
                )
